import numpy as np
import ml_dtypes


def mxq(x, axis, fmt="e4m3"):
    dtype, down = {"e4m3": (ml_dtypes.float8_e4m3fn, 7), "e5m2": (ml_dtypes.float8_e5m2, 14)}[fmt]
    v = np.moveaxis(np.asarray(x, np.float32).astype(ml_dtypes.bfloat16).astype(np.float64), axis, -1)
    blocks = v.reshape(v.shape[:-1] + (-1, 32))
    amax = np.abs(blocks).max(-1, keepdims=True)
    byte = np.maximum(np.where(amax > 0, np.frexp(amax)[1] - 1 + 127, 0) - down, 1)
    scale = np.exp2(byte - 127.0)
    codes = (blocks / scale).astype(np.float32).astype(dtype).astype(np.float64)
    return np.moveaxis((codes * scale).reshape(v.shape), -1, axis)


WIDE = False


def mx_kscale(k):
    if not WIDE:
        return np.ones(k)
    levels = np.array([10, -10, 5, -5, 0])
    if k % 512:
        return np.exp2(np.random.permutation(np.resize(levels, k // 32))).repeat(32)
    a = np.empty((k // 512, 16))
    for p in range(k // 512):
        a[p, :8] = np.random.permutation(np.resize(levels, 8))
        for g in range(8):
            far = levels[np.abs(levels - a[p, g]) >= 10]
            a[p, g + 8] = far[np.random.randint(len(far))]
    return np.exp2(a.ravel()).repeat(32)


def f64(x):
    return np.asarray(x).astype(np.float64)


def striped(idx):
    return np.tile(idx.reshape(-1, 16).T, (8, 1)).astype(np.uint16)


def unstriped(offs):
    return offs[:16].T.reshape(-1).astype(np.int64)


def striped8(idx):
    return np.concatenate([x.reshape(-1, 16).T for x in idx]).astype(np.uint16)


def runs(offs, k):
    lists = np.stack([offs[16 * r : 16 * r + 16].T.reshape(-1) for r in range(8)]).astype(np.int64)
    return lists[np.arange(k) % 512 // 64]


def pack_weight(w):
    k, n = w.shape
    w = f64(np.asarray(w, np.float32).astype(ml_dtypes.bfloat16)).reshape(k // 32, 32, n)
    amax = np.abs(w).max(1)
    byte = np.clip(np.where(amax > 0, np.frexp(amax)[1] - 1 + 127 - 7, 1), 1, 254)
    scaled = (w * np.exp2(127.0 - byte)[:, None, :]).reshape(k, n).astype(np.float32)
    words = np.ascontiguousarray(scaled.reshape(k // 512, 128, 4, n).transpose(0, 1, 3, 2)).astype(ml_dtypes.float8_e4m3fn).view(np.uint8)
    return words, np.ascontiguousarray(byte.astype(np.uint8).reshape(k // 512, 16, n))


def unpack_weight(words, scales):
    g, p, n, _ = words.shape
    vals = np.ascontiguousarray(words).view(ml_dtypes.float8_e4m3fn).astype(np.float64) * np.repeat(np.exp2(scales.astype(np.float64) - 127.0), 8, axis=1)[..., None]
    return vals.transpose(0, 1, 3, 2).reshape(g * 512, n)

def planes(y):
    n, m = y.shape
    v = y.astype(np.float32).astype(ml_dtypes.bfloat16).astype(np.float64).reshape(n // 32, 32, m)
    top = np.abs(v).max(1)
    byte = np.clip(np.where(top > 0, np.frexp(top)[1] - 1 + 127 - 7, 1), 1, 254)
    codes = (v * np.exp2(127.0 - byte)[:, None, :]).reshape(n, m).astype(np.float32).astype(ml_dtypes.float8_e4m3fn).view(np.uint8)
    words = codes.reshape(n // 512, 128, 4, m).transpose(0, 1, 3, 2)
    return np.ascontiguousarray(words), np.ascontiguousarray(byte.astype(np.uint8).reshape(n // 512, 16, m))


K, T, S, N, H = 512, 2048, 256, 512, 512


def setup_inputs():
    n = np.random.standard_normal
    s = mx_kscale(K)[:, None]
    u = mx_kscale(H)
    packed_xT = pack_weight(n((K, T)) * s)
    packed_w1 = pack_weight(n((K, H)) / np.sqrt(K) / s)
    packed_w2 = pack_weight(n((K, H)) / np.sqrt(K) / s)
    packed_w3 = pack_weight(n((H, N)) / np.sqrt(2 * H) / u[:, None])
    packed_w4 = pack_weight(n((H, N)) / np.sqrt(2 * H) / u[:, None])
    return {
        "x_words": packed_xT[0],
        "x_scales": packed_xT[1],
        "w1_words": packed_w1[0],
        "w1_scales": packed_w1[1],
        "w2_words": packed_w2[0],
        "w2_scales": packed_w2[1],
        "tau": np.random.uniform(0.3, 0.9, (H, 1)).astype(np.float32),
        "gn": (np.random.uniform(0.5, 1.5, (H, 1)) * u[:, None]).astype(np.float32),
        "gm": (np.random.uniform(0.5, 1.5, (H, 1)) * u[:, None]).astype(np.float32),
        "w3_words": packed_w3[0],
        "w3_scales": packed_w3[1],
        "w4_words": packed_w4[0],
        "w4_scales": packed_w4[1],
        "tau2": np.random.uniform(0.3, 0.9, (N, 1)).astype(np.float32),
        "offs": striped(np.random.permutation(T)[:S]),
        "hz": striped8(np.random.randint(0, T, (8, S))),
        "n1": striped(np.random.permutation(S)),
        "n2": striped(np.random.permutation(S)),
        "n3": striped(np.random.permutation(S)),
        "n4": striped(np.random.permutation(S)),
        "n5": striped(np.random.permutation(S)),
        "n6": striped(np.random.permutation(S)),
    }


def reference(x_words, x_scales, w1_words, w1_scales, w2_words, w2_scales, tau, gn, gm, w3_words, w3_scales, w4_words, w4_scales, tau2, offs, hz, n1, n2, n3, n4, n5, n6):
    xq = unpack_weight(x_words, x_scales)[:, unstriped(offs)]
    y = unpack_weight(w1_words, w1_scales).T @ xq
    st = y - y[:, unstriped(n1)]
    su = np.maximum(st, st[:, unstriped(n2)])
    z = f64(gn) * (su + 0.5 * su[:, unstriped(n3)])
    x_hz = unpack_weight(x_words, x_scales)[np.arange(K)[:, None], runs(hz, K)]
    d = unpack_weight(w2_words, w2_scales).T @ x_hz
    top = d.max(axis=1, keepdims=True)
    ea = np.exp(f64(tau) * (d[:, unstriped(n4)] - top))
    z2 = f64(gm) * (2.0 * (d * ea))
    h = unpack_weight(w3_words, w3_scales).T @ mxq(z, 0, "e4m3") + unpack_weight(w4_words, w4_scales).T @ mxq(z2, 0, "e4m3")
    top2 = h.max(axis=1, keepdims=True)
    ea2 = np.exp(f64(tau2) * (h[:, unstriped(n5)] - top2))
    out_0 = np.maximum(h, 2.0 * ea2) - (0.5 * h[:, unstriped(n6)])
    return (out_0,) + planes(out_0)

@@ -1,0 +1,252 @@
+from contextlib import ExitStack
+
+import concourse.mybir as mybir
+
+K, T, S, N, H = 512, 2048, 256, 512, 512
+FLOPS = 2 * K * H * S * 2 + 2 * H * N * S * 2
+
+F32 = mybir.dt.float32
+BF16 = mybir.dt.bfloat16
+I32 = mybir.dt.int32
+U32 = mybir.dt.uint32
+U16 = mybir.dt.uint16
+U8 = mybir.dt.uint8
+FP8X4 = mybir.dt.float8_e4m3fn_x4
+ALU = mybir.AluOpType
+ACT = mybir.ActivationFunctionType
+
+P = 128
+PACK = 4
+QUADS = 4
+
+
+def tile_picked_hjointhreeepkecl_none_po_kernel(
+    tc, x_words, x_scales, w1_words, w1_scales, w2_words, w2_scales, tau, gn, gm,
+    w3_words, w3_scales, w4_words, w4_scales, tau2, offs, hz, n1, n2, n3, n4, n5, n6,
+    out_0, out_1, out_2,
+):
+    nc = tc.nc
+    with ExitStack() as ctx:
+        lists = ctx.enter_context(tc.tile_pool(name="lists", bufs=1))
+        sb = ctx.enter_context(tc.tile_pool(name="sb", bufs=1))
+        psum = ctx.enter_context(tc.psum_pool(name="psum", bufs=1))
+
+        def load_list(src, name):
+            tile = lists.tile([P, S // 16], U16, name=name)
+            nc.sync.dma_start(tile[:], src)
+            return tile
+
+        def load_words(src, width, name):
+            tile = sb.tile([P, width], U32, name=name, align_bytes=64)
+            nc.sync.dma_start(tile[:].bitcast(I32), src[0].rearrange("p n t -> p (n t)").bitcast(I32))
+            return tile
+
+        def load_column(src, name):
+            tile = sb.tile([P, PACK], F32, name=name)
+            nc.gpsimd.dma_start(tile[:], src.rearrange("(p t) o -> p (t o)", t=PACK))
+            return tile
+
+        def load_scale_rows(tile, src, engine, copies):
+            for q in range(QUADS):
+                rows = src[0, 4 * q:4 * q + 4, :].bitcast(I32)
+                if copies > 1:
+                    rows = rows.unsqueeze(0).broadcast_to([copies] + list(rows.shape))
+                engine.dma_start(tile[32 * q:32 * q + 4 * copies, :].bitcast(I32), rows)
+
+        def deal_bytes(engine, raw, name):
+            tile = sb.tile([P, H], U8, name=name, align_bytes=64)
+            engine.tensor_copy(tile[:].rearrange("p (t m) -> p t m", t=PACK), raw[:].rearrange("p (m t) -> p t m", t=PACK))
+            return tile
+
+        def deal_words(engine, raw, name):
+            tile = sb.tile([P, H], U32, name=name, align_bytes=64)
+            dst = tile[:].rearrange("p (t a i) -> p a t i", t=PACK, i=4)
+            src = raw[:].rearrange("p (a i t) -> p a t i", t=PACK, i=4)
+            if engine == "s":
+                nc.scalar.copy(dst, src)
+            else:
+                nc.gpsimd.tensor_copy(dst, src)
+            return tile
+
+        xs = sb.tile([P, T], U8, name="xs", align_bytes=64)
+        load_scale_rows(xs, x_scales, nc.scalar, 8)
+        offs_t = load_list(offs, "offs_t")
+        xw = load_words(x_words, T, "xw")
+        w1r = load_words(w1_words, H, "w1r")
+        hz_t = load_list(hz, "hz_t")
+        wsa = sb.tile([P, H], U8, name="wsa", align_bytes=64)
+        load_scale_rows(wsa, w1_scales, nc.scalar, 8)
+        n1_t = load_list(n1, "n1_t")
+        w2r = load_words(w2_words, H, "w2r")
+        wsb = sb.tile([P, H], U8, name="wsb", align_bytes=64)
+        load_scale_rows(wsb, w2_scales, nc.sync, 8)
+
+        tau_t = load_column(tau, "tau_t")
+        gn_t = load_column(gn, "gn_t")
+        gm_t = load_column(gm, "gm_t")
+
+        ywin = [sb.tile([P, 2 * S], F32, name=f"ywin{t}") for t in range(PACK)]
+        dwin = [sb.tile([P, 2 * S], F32, name=f"dwin{t}") for t in range(PACK)]
+        for tile in ywin + dwin[1:]:
+            nc.vector.memset(tile[:, S:], 0.0)
+        nc.scalar.activation(dwin[0][:, S:], ywin[0][:, S:], ACT.Copy)
+
+        xs1 = sb.tile([P, S], U8, name="xs1", align_bytes=64)
+        nc.vector.tensor_copy(xs1[:], xs[:].indirect(offs_t[:]))
+        w1s = deal_bytes(nc.vector, wsa, "w1s")
+        xg1 = sb.tile([P, S], U32, name="xg1", align_bytes=64)
+        nc.vector.tensor_copy(xg1[:], xw[:].indirect(offs_t[:]))
+        w1d = deal_words("s", w1r, "w1d")
+
+        xs2g = sb.tile([P, S], U8, name="xs2g", align_bytes=64)
+        nc.vector.tensor_copy(xs2g[:], xs[:].indirect(hz_t[:]))
+        xs2 = sb.tile([P, S], U8, name="xs2", align_bytes=64)
+        nc.vector.tensor_copy(xs2[:], xs2g[:])
+        for r in (2, 3):
+            nc.sync.dma_start(xs2[r:P:32, :].bitcast(I32), xs2g[16 + r:P:32, :].bitcast(I32))
+        xg2 = sb.tile([P, S], U32, name="xg2", align_bytes=64)
+        nc.vector.tensor_copy(xg2[:], xw[:].indirect(hz_t[:]))
+        w2d = deal_words("g", w2r, "w2d")
+        w2s = deal_bytes(nc.gpsimd, wsb, "w2s")
+
+        n2_t = load_list(n2, "n2_t")
+        n3_t = load_list(n3, "n3_t")
+        n4_t = load_list(n4, "n4_t")
+        n6_t = load_list(n6, "n6_t")
+        n5_t = load_list(n5, "n5_t")
+        tau2_t = sb.tile([P, PACK], F32, name="tau2_t")
+        nc.sync.dma_start(tau2_t[:], tau2.rearrange("(p t) o -> p (t o)", t=PACK))
+
+        nc.sync.dma_start(w1r[:].bitcast(I32), w3_words[0].rearrange("p n t -> p (n t)").bitcast(I32))
+        load_scale_rows(wsa, w3_scales, nc.sync, 1)
+        nc.sync.dma_start(w2r[:].bitcast(I32), w4_words[0].rearrange("p n t -> p (n t)").bitcast(I32))
+        load_scale_rows(wsb, w4_scales, nc.sync, 1)
+        w3d = deal_words("g", w1r, "w3d")
+        w3s = deal_bytes(nc.gpsimd, wsa, "w3s")
+        w4d = deal_words("g", w2r, "w4d")
+        w4s = deal_bytes(nc.gpsimd, wsb, "w4s")
+
+        gm2 = sb.tile([P, PACK], F32, name="gm2")
+        nc.gpsimd.tensor_scalar(gm2[:], gm_t[:], 2.0, 0.0, ALU.mult, ALU.add)
+
+        def product(bank, words, plane, t, rhs, rhs_plane, start, stop):
+            cols = slice(t * P, (t + 1) * P)
+            nc.tensor.matmul_mx(bank[:], lhsT=words[:, cols].bitcast(FP8X4), lhsT_scale=plane[:, cols],
+                                rhs=rhs.bitcast(FP8X4), rhs_scale=rhs_plane, start=start, stop=stop)
+
+        yb = [psum.tile([P, S], F32, name=f"yb{t}", tag=f"a{t}") for t in range(PACK)]
+        db = [psum.tile([P, S], F32, name=f"db{t}", tag=f"b{t}") for t in range(PACK)]
+        for t in range(PACK):
+            product(yb[t], w1d, w1s, t, xg1[:], xs1[:], True, True)
+        for t in range(PACK):
+            product(db[t], w2d, w2s, t, xg2[:], xs2[:], True, True)
+
+        def gather(engine, out, window, offsets):
+            if engine == "v":
+                nc.vector.tensor_copy(out, window.indirect(offsets[:]))
+            else:
+                nc.scalar.activation(out, window.indirect(offsets[:]), ACT.Copy)
+
+        def leave_with_top(bank, win, top, nrate, bias, t):
+            nc.vector.tensor_scalar(win[:, :S], bank[:], 1.0, None, ALU.mult, ALU.max, accum_out=top[:, t:t + 1])
+            nc.vector.tensor_scalar(bias[:, t:t + 1], top[:, t:t + 1], nrate[:, t:t + 1], -1.0, ALU.mult, ALU.mult)
+
+        stw = [sb.tile([P, 2 * S], F32, name=f"stw{t}") for t in range(PACK)]
+        g2 = sb.tile([P, PACK, S], F32, name="g2")
+        zw = sb.tile([P, PACK, 2 * S], F32, name="zw")
+        g3 = sb.tile([P, PACK, S], F32, name="g3")
+        ea = sb.tile([P, PACK, S], F32, name="ea")
+        z2f = sb.tile([P, PACK, S], F32, name="z2f")
+        top = sb.tile([P, PACK], F32, name="top")
+        bias = sb.tile([P, PACK], F32, name="bias")
+
+        zb = sb.tile([P, PACK * S], BF16, name="zb", align_bytes=64)
+        zq = sb.tile([P, S], U32, name="zq", align_bytes=64)
+        zs = sb.tile([P, S], U8, name="zs", align_bytes=64)
+
+        def ev(t):
+            nc.scalar.copy(ywin[t][:, :S], yb[t][:])
+
+        def g1(t):
+            gather("s", stw[t][:, S:], ywin[t][:], n1_t)
+
+        def sub(t):
+            nc.vector.tensor_tensor(stw[t][:, :S], yb[t][:], stw[t][:, S:], ALU.subtract)
+
+        def dev(t):
+            leave_with_top(db[t], dwin[t], top, tau_t, bias, t)
+
+        def gg2(t):
+            gather("v" if t < 2 else "s", g2[:, t, :], stw[t][:], n2_t)
+
+        def mx(t):
+            nc.vector.tensor_tensor(zw[:, t, S:], stw[t][:, :S], g2[:, t, :], ALU.max)
+
+        def ts(t):
+            nc.vector.tensor_scalar(zw[:, t, :S], zw[:, t, S:], gn_t[:, t:t + 1], None, ALU.mult)
+
+        def gg3(t):
+            nc.scalar.activation(g3[:, t, :], zw[:, t, :].indirect(n3_t[:]), ACT.Copy, scale=0.5)
+
+        def ex(t):
+            nc.scalar.activation(ea[:, t, :], dwin[t][:].indirect(n4_t[:]), ACT.Exp,
+                                 bias=bias[:, t:t + 1], scale=tau_t[:, t:t + 1])
+
+        def stt(t):
+            nc.vector.scalar_tensor_tensor(z2f[:, t, :], db[t][:], gm2[:, t:t + 1], ea[:, t, :], ALU.mult, ALU.mult)
+
+        def interleave(src, name):
+            tile = sb.tile([P, PACK * S], BF16, name=name, align_bytes=64)
+            nc.vector.tensor_copy(tile[:].rearrange("p (c i t) -> p c t i", i=4, t=PACK),
+                                  src[:].rearrange("p t (c i) -> p c t i", i=4))
+            return tile
+
+        ev(0), ev(1), g1(0), ev(2), g1(1), ev(3), g1(2), g1(3)
+        sub(0), gg2(0), sub(1), mx(0), gg2(1), sub(2), ts(0), mx(1), sub(3), ts(1), dev(0), dev(1)
+        gg2(2), gg2(3), gg3(0), gg3(1)
+        mx(2), mx(3), ts(2), ts(3), dev(2), dev(3)
+        ex(0), ex(1), gg3(2), gg3(3), stt(0), stt(1)
+        nc.vector.tensor_tensor(
+            zb[:].rearrange("p (c i t) -> p c t i", i=4, t=PACK),
+            zw[:, :, :S].rearrange("p t (c i) -> p c t i", i=4),
+            g3[:].rearrange("p t (c i) -> p c t i", i=4), ALU.add)
+        ex(2), ex(3), stt(2)
+        nc.vector.quantize_mx(out=zq[:].bitcast(FP8X4), scales=zs[:], in_=zb[:])
+        stt(3)
+        hb = [psum.tile([P, S], F32, name=f"hb{t}", tag=f"a{t}") for t in range(PACK)]
+        for t in range(PACK):
+            product(hb[t], w3d, w3s, t, zq[:], zs[:], True, False)
+
+        z2b = interleave(z2f, "z2b")
+        z2q = sb.tile([P, S], U32, name="z2q", align_bytes=64)
+        z2s = sb.tile([P, S], U8, name="z2s", align_bytes=64)
+        nc.vector.quantize_mx(out=z2q[:].bitcast(FP8X4), scales=z2s[:], in_=z2b[:])
+        for t in range(PACK):
+            product(hb[t], w4d, w4s, t, z2q[:], z2s[:], False, True)
+
+        hwin = ywin
+        top2 = sb.tile([P, PACK], F32, name="top2")
+        bias2 = sb.tile([P, PACK], F32, name="bias2")
+        g6 = sb.tile([P, PACK, S], F32, name="g6")
+        ea2 = sb.tile([P, PACK, S], F32, name="ea2")
+        big = sb.tile([P, PACK, S], F32, name="big")
+        res = sb.tile([P, PACK, S], F32, name="res")
+        out_rows = out_0.rearrange("(p t) c -> p t c", t=PACK)
+        for t in range(PACK):
+            leave_with_top(hb[t], hwin[t], top2, tau2_t, bias2, t)
+        for t in range(PACK):
+            gather("v" if t == 3 else "s", g6[:, t, :], hwin[t][:], n6_t)
+            nc.scalar.activation(ea2[:, t, :], hwin[t][:].indirect(n5_t[:]), ACT.Exp,
+                                 bias=bias2[:, t:t + 1], scale=tau2_t[:, t:t + 1])
+            nc.vector.scalar_tensor_tensor(big[:, t, :], ea2[:, t, :], 2.0, hb[t][:], ALU.mult, ALU.max)
+            nc.vector.scalar_tensor_tensor(res[:, t, :], g6[:, t, :], -0.5, big[:, t, :], ALU.mult, ALU.add)
+            nc.sync.dma_start(out_rows[:, t, :], res[:, t, :])
+
+        ob = interleave(res, "ob")
+        oq = sb.tile([P, S], U32, name="oq", align_bytes=64)
+        osc = sb.tile([P, S], U8, name="osc", align_bytes=64)
+        nc.vector.quantize_mx(out=oq[:].bitcast(FP8X4), scales=osc[:], in_=ob[:])
+        nc.sync.dma_start(out_1[0].rearrange("p n t -> p (n t)").bitcast(I32), oq[:].bitcast(I32))
+        for q in range(QUADS):
+            engine = nc.scalar if q % 2 == 0 else nc.sync
+            engine.dma_start(out_2[0, 4 * q:4 * q + 4, :].bitcast(I32), osc[32 * q:32 * q + 4, :].bitcast(I32))

@@ -3,7 +3,7 @@ from contextlib import ExitStack
 import concourse.mybir as mybir
 
 K, T, S, N, H = 512, 2048, 256, 512, 512
-FLOPS = 2 * K * H * S * 2 + 2 * H * N * S * 2
+FLOPS = 2 * (2 * K * H * S) + 2 * (2 * H * N * S)
 
 F32 = mybir.dt.float32
 BF16 = mybir.dt.bfloat16
@@ -18,6 +18,10 @@ ACT = mybir.ActivationFunctionType
 P = 128
 PACK = 4
 QUADS = 4
+LINE = 4
+FILL = 8
+TILES = range(PACK)
+PAIRS = ((0, 1), (2, 3))
 
 
 def tile_picked_hjointhreeepkecl_none_po_kernel(
@@ -37,216 +41,226 @@ def tile_picked_hjointhreeepkecl_none_po_kernel(
             return tile
 
         def load_words(src, width, name):
-            tile = sb.tile([P, width], U32, name=name, align_bytes=64)
+            tile = sb.tile([P, width], U32, name=name, tag=name, align_bytes=64)
             nc.sync.dma_start(tile[:].bitcast(I32), src[0].rearrange("p n t -> p (n t)").bitcast(I32))
             return tile
 
-        def load_column(src, name):
+        def load_row_values(queue, src, name):
             tile = sb.tile([P, PACK], F32, name=name)
-            nc.gpsimd.dma_start(tile[:], src.rearrange("(p t) o -> p (t o)", t=PACK))
+            queue.dma_start(tile[:], src.rearrange("(p t) o -> p (t o)", t=PACK))
             return tile
 
-        def load_scale_rows(tile, src, engine, copies):
-            for q in range(QUADS):
+        def fill_scale_rows(tile, src, queues):
+            for q, queue in enumerate(queues):
                 rows = src[0, 4 * q:4 * q + 4, :].bitcast(I32)
-                if copies > 1:
-                    rows = rows.unsqueeze(0).broadcast_to([copies] + list(rows.shape))
-                engine.dma_start(tile[32 * q:32 * q + 4 * copies, :].bitcast(I32), rows)
+                queue.dma_start(tile[32 * q:32 * (q + 1), :].bitcast(I32),
+                                rows.unsqueeze(0).broadcast_to([FILL] + list(rows.shape)))
 
-        def deal_bytes(engine, raw, name):
-            tile = sb.tile([P, H], U8, name=name, align_bytes=64)
-            engine.tensor_copy(tile[:].rearrange("p (t m) -> p t m", t=PACK), raw[:].rearrange("p (m t) -> p t m", t=PACK))
-            return tile
+        def load_scale_rows(tile, src, first):
+            for q in range(QUADS):
+                nc.sync.dma_start(tile[32 * q + first:32 * q + first + 4, :].bitcast(I32),
+                                  src[0, 4 * q:4 * q + 4, :].bitcast(I32))
 
-        def deal_words(engine, raw, name):
+        def dealt_views(dealt, raw):
+            return (dealt[:].rearrange("p (t a i) -> p a t i", t=PACK, i=LINE),
+                    raw[:].rearrange("p (a i t) -> p a t i", t=PACK, i=LINE))
+
+        def deal_words(raw, name):
             tile = sb.tile([P, H], U32, name=name, align_bytes=64)
-            dst = tile[:].rearrange("p (t a i) -> p a t i", t=PACK, i=4)
-            src = raw[:].rearrange("p (a i t) -> p a t i", t=PACK, i=4)
-            if engine == "s":
-                nc.scalar.copy(dst, src)
-            else:
-                nc.gpsimd.tensor_copy(dst, src)
+            nc.gpsimd.tensor_copy(*dealt_views(tile, raw))
             return tile
 
-        xs = sb.tile([P, T], U8, name="xs", align_bytes=64)
-        load_scale_rows(xs, x_scales, nc.scalar, 8)
-        offs_t = load_list(offs, "offs_t")
-        xw = load_words(x_words, T, "xw")
-        w1r = load_words(w1_words, H, "w1r")
-        hz_t = load_list(hz, "hz_t")
-        wsa = sb.tile([P, H], U8, name="wsa", align_bytes=64)
-        load_scale_rows(wsa, w1_scales, nc.scalar, 8)
-        n1_t = load_list(n1, "n1_t")
-        w2r = load_words(w2_words, H, "w2r")
-        wsb = sb.tile([P, H], U8, name="wsb", align_bytes=64)
-        load_scale_rows(wsb, w2_scales, nc.sync, 8)
+        def deal_bytes(raw, name, tag):
+            tile = sb.tile([P, H], U8, name=name, tag=tag, align_bytes=64)
+            nc.gpsimd.tensor_copy(tile[:].rearrange("p (t m) -> p t m", t=PACK),
+                                  raw[:].rearrange("p (m t) -> p t m", t=PACK))
+            return tile
 
-        tau_t = load_column(tau, "tau_t")
-        gn_t = load_column(gn, "gn_t")
-        gm_t = load_column(gm, "gm_t")
+        def gather_packed(out, window, offsets):
+            nc.vector.tensor_copy(out[:], window[:].indirect(offsets[:]))
 
-        ywin = [sb.tile([P, 2 * S], F32, name=f"ywin{t}") for t in range(PACK)]
-        dwin = [sb.tile([P, 2 * S], F32, name=f"dwin{t}") for t in range(PACK)]
-        for tile in ywin + dwin[1:]:
+        shared_queues = (nc.scalar, nc.scalar, nc.scalar, nc.sync)
+        x_rows = sb.tile([P, T], U8, name="x_rows", align_bytes=64)
+        fill_scale_rows(x_rows, x_scales, shared_queues)
+        offs_list = load_list(offs, "offs_list")
+        hz_list = load_list(hz, "hz_list")
+        x_table = load_words(x_words, T, "x_table")
+        w1_rows = sb.tile([P, H], U8, name="w1_rows", align_bytes=64)
+        fill_scale_rows(w1_rows, w1_scales, shared_queues)
+        n1_list = load_list(n1, "n1_list")
+        w1_raw = load_words(w1_words, H, "w1_raw")
+        w2_raw = load_words(w2_words, H, "w2_raw")
+        n2_list = load_list(n2, "n2_list")
+        w2_rows = sb.tile([P, H], U8, name="w2_rows", align_bytes=64)
+        fill_scale_rows(w2_rows, w2_scales, (nc.sync,) * QUADS)
+        w3_raw = load_words(w3_words, N, "w3_raw")
+        w4_raw = load_words(w4_words, N, "w4_raw")
+        tau_rows = load_row_values(nc.gpsimd, tau, "tau_rows")
+        gn_rows = load_row_values(nc.gpsimd, gn, "gn_rows")
+        gm_rows = load_row_values(nc.gpsimd, gm, "gm_rows")
+
+        y_win = [sb.tile([P, 2 * S], F32, name=f"y_win{t}") for t in TILES]
+        d_win = [sb.tile([P, 2 * S], F32, name=f"d_win{t}", align_bytes=64) for t in TILES]
+        for tile in y_win + d_win:
             nc.vector.memset(tile[:, S:], 0.0)
-        nc.scalar.activation(dwin[0][:, S:], ywin[0][:, S:], ACT.Copy)
 
-        xs1 = sb.tile([P, S], U8, name="xs1", align_bytes=64)
-        nc.vector.tensor_copy(xs1[:], xs[:].indirect(offs_t[:]))
-        w1s = deal_bytes(nc.vector, wsa, "w1s")
-        xg1 = sb.tile([P, S], U32, name="xg1", align_bytes=64)
-        nc.vector.tensor_copy(xg1[:], xw[:].indirect(offs_t[:]))
-        w1d = deal_words("s", w1r, "w1d")
+        picked_plane = sb.tile([P, S], U8, name="picked_plane", align_bytes=64)
+        gather_packed(picked_plane, x_rows, offs_list)
+        w1_plane = deal_bytes(w1_rows, "w1_plane", "w1_plane")
+        picked_words = sb.tile([P, S], U32, name="picked_words", align_bytes=64)
+        gather_packed(picked_words, x_table, offs_list)
+        w1_dealt = sb.tile([P, H], U32, name="w1_dealt", align_bytes=64)
+        dealt_view, raw_view = dealt_views(w1_dealt, w1_raw)
+        for a, b in PAIRS:
+            nc.scalar.copy(dealt_view[:, :, a:b + 1, :], raw_view[:, :, a:b + 1, :])
 
-        xs2g = sb.tile([P, S], U8, name="xs2g", align_bytes=64)
-        nc.vector.tensor_copy(xs2g[:], xs[:].indirect(hz_t[:]))
-        xs2 = sb.tile([P, S], U8, name="xs2", align_bytes=64)
-        nc.vector.tensor_copy(xs2[:], xs2g[:])
+        hashed_bytes = sb.tile([P, S], U8, name="hashed_bytes", align_bytes=64)
+        gather_packed(hashed_bytes, x_rows, hz_list)
+        hashed_plane = sb.tile([P, S], U8, name="hashed_plane", align_bytes=64)
+        nc.vector.tensor_copy(hashed_plane[:], hashed_bytes[:])
         for r in (2, 3):
-            nc.sync.dma_start(xs2[r:P:32, :].bitcast(I32), xs2g[16 + r:P:32, :].bitcast(I32))
-        xg2 = sb.tile([P, S], U32, name="xg2", align_bytes=64)
-        nc.vector.tensor_copy(xg2[:], xw[:].indirect(hz_t[:]))
-        w2d = deal_words("g", w2r, "w2d")
-        w2s = deal_bytes(nc.gpsimd, wsb, "w2s")
+            nc.sync.dma_start(hashed_plane[r:P:32, :].bitcast(I32), hashed_bytes[16 + r:P:32, :].bitcast(I32))
+        hashed_words = sb.tile([P, S], U32, name="hashed_words", align_bytes=64)
+        gather_packed(hashed_words, x_table, hz_list)
+        w2_dealt = deal_words(w2_raw, "w2_dealt")
+        w2_plane = deal_bytes(w2_rows, "w2_plane", "w2_raw")
 
-        n2_t = load_list(n2, "n2_t")
-        n3_t = load_list(n3, "n3_t")
-        n4_t = load_list(n4, "n4_t")
-        n6_t = load_list(n6, "n6_t")
-        n5_t = load_list(n5, "n5_t")
-        tau2_t = sb.tile([P, PACK], F32, name="tau2_t")
-        nc.sync.dma_start(tau2_t[:], tau2.rearrange("(p t) o -> p (t o)", t=PACK))
+        n3_list = load_list(n3, "n3_list")
+        n4_list = load_list(n4, "n4_list")
+        n6_list = load_list(n6, "n6_list")
+        n5_list = load_list(n5, "n5_list")
+        tau2_rows = load_row_values(nc.sync, tau2, "tau2_rows")
 
-        nc.sync.dma_start(w1r[:].bitcast(I32), w3_words[0].rearrange("p n t -> p (n t)").bitcast(I32))
-        load_scale_rows(wsa, w3_scales, nc.sync, 1)
-        nc.sync.dma_start(w2r[:].bitcast(I32), w4_words[0].rearrange("p n t -> p (n t)").bitcast(I32))
-        load_scale_rows(wsb, w4_scales, nc.sync, 1)
-        w3d = deal_words("g", w1r, "w3d")
-        w3s = deal_bytes(nc.gpsimd, wsa, "w3s")
-        w4d = deal_words("g", w2r, "w4d")
-        w4s = deal_bytes(nc.gpsimd, wsb, "w4s")
+        w3_dealt = deal_words(w3_raw, "w3_dealt")
+        w4_dealt = deal_words(w4_raw, "w4_dealt")
+        load_scale_rows(w1_rows, w3_scales, 0)
+        load_scale_rows(w1_rows, w4_scales, 4)
+        w34_planes = deal_bytes(w1_rows, "w34_planes", "w34_planes")
 
-        gm2 = sb.tile([P, PACK], F32, name="gm2")
-        nc.gpsimd.tensor_scalar(gm2[:], gm_t[:], 2.0, 0.0, ALU.mult, ALU.add)
-
-        def product(bank, words, plane, t, rhs, rhs_plane, start, stop):
+        def product(bank, words, plane, t, moving, moving_plane, start, stop):
             cols = slice(t * P, (t + 1) * P)
             nc.tensor.matmul_mx(bank[:], lhsT=words[:, cols].bitcast(FP8X4), lhsT_scale=plane[:, cols],
-                                rhs=rhs.bitcast(FP8X4), rhs_scale=rhs_plane, start=start, stop=stop)
+                                rhs=moving[:].bitcast(FP8X4), rhs_scale=moving_plane[:], start=start, stop=stop)
 
-        yb = [psum.tile([P, S], F32, name=f"yb{t}", tag=f"a{t}") for t in range(PACK)]
-        db = [psum.tile([P, S], F32, name=f"db{t}", tag=f"b{t}") for t in range(PACK)]
-        for t in range(PACK):
-            product(yb[t], w1d, w1s, t, xg1[:], xs1[:], True, True)
-        for t in range(PACK):
-            product(db[t], w2d, w2s, t, xg2[:], xs2[:], True, True)
+        y_bank = [psum.tile([P, S], F32, name=f"y_bank{t}", tag=f"first{t}") for t in TILES]
+        d_bank = [psum.tile([P, S], F32, name=f"d_bank{t}") for t in TILES]
+        for t in TILES:
+            product(y_bank[t], w1_dealt, w1_plane, t, picked_words, picked_plane, True, True)
+        for t in TILES:
+            product(d_bank[t], w2_dealt, w2_plane, t, hashed_words, hashed_plane, True, True)
 
-        def gather(engine, out, window, offsets):
-            if engine == "v":
-                nc.vector.tensor_copy(out, window.indirect(offsets[:]))
-            else:
-                nc.scalar.activation(out, window.indirect(offsets[:]), ACT.Copy)
+        def leave_with_bias(bank, win, rate, top, bias, t):
+            col = slice(t, t + 1)
+            nc.vector.tensor_scalar(win[:, :S], bank[:], 1.0, None, ALU.mult, ALU.max, accum_out=top[:, col])
+            nc.gpsimd.tensor_scalar(bias[:, col], top[:, col], rate[:, col], -1.0, ALU.mult, ALU.mult)
 
-        def leave_with_top(bank, win, top, nrate, bias, t):
-            nc.vector.tensor_scalar(win[:, :S], bank[:], 1.0, None, ALU.mult, ALU.max, accum_out=top[:, t:t + 1])
-            nc.vector.tensor_scalar(bias[:, t:t + 1], top[:, t:t + 1], nrate[:, t:t + 1], -1.0, ALU.mult, ALU.mult)
+        def gather_exp(out, win, offsets, rate, bias, t):
+            nc.scalar.activation(out, win[:].indirect(offsets[:]), ACT.Exp,
+                                 bias=bias[:, t:t + 1], scale=rate[:, t:t + 1])
 
-        stw = [sb.tile([P, 2 * S], F32, name=f"stw{t}") for t in range(PACK)]
-        g2 = sb.tile([P, PACK, S], F32, name="g2")
-        zw = sb.tile([P, PACK, 2 * S], F32, name="zw")
-        g3 = sb.tile([P, PACK, S], F32, name="g3")
+        def interleaved(tile):
+            return tile[:].rearrange("p (c i t) -> p c t i", i=LINE, t=PACK)
+
+        def by_lines(tiles):
+            return tiles.rearrange("p t (c i) -> p c t i", i=LINE)
+
+        def quantise_by_halves(src, factor, name):
+            codes = sb.tile([P, S], U32, name=name + "_codes", align_bytes=64)
+            plane = sb.tile([P, S], U8, name=name + "_plane", align_bytes=64)
+            low = sb.tile([P, PACK * S // 2], BF16, name=name + "_low", align_bytes=64)
+            nc.vector.tensor_scalar(interleaved(low), by_lines(src[:, :, :S // 2]), factor, None, ALU.mult)
+            high = sb.tile([P, PACK * S // 2], BF16, name=name + "_high", align_bytes=64)
+            nc.scalar.activation(interleaved(high), by_lines(src[:, :, S // 2:]), ACT.Copy, scale=factor)
+            for rounded, cols in ((low, slice(0, S // 2)), (high, slice(S // 2, S))):
+                nc.vector.quantize_mx(out=codes[:, cols].bitcast(FP8X4), scales=plane[:, cols], in_=rounded[:])
+            return codes, plane
+
+        st_win = [sb.tile([P, 2 * S], F32, name=f"st_win{t}") for t in TILES]
+        for a, b in PAIRS:
+            nc.scalar.copy(y_win[a][:, :S], y_bank[a][:])
+            nc.scalar.copy(y_win[b][:, :S], y_bank[b][:])
+            nc.scalar.activation(st_win[a][:, S:], y_win[a][:].indirect(n1_list[:]), ACT.Copy)
+            nc.vector.tensor_copy(st_win[b][:, S:], y_win[b][:].indirect(n1_list[:]))
+            for t in (a, b):
+                nc.vector.tensor_tensor(st_win[t][:, :S], y_bank[t][:], st_win[t][:, S:], ALU.subtract)
+
+        gained = sb.tile([P, PACK, 2 * S], F32, name="gained")
+        for t in TILES:
+            nc.scalar.activation(gained[:, t, S:], st_win[t][:].indirect(n2_list[:]), ACT.Copy)
+        for pair in PAIRS:
+            for t in pair:
+                nc.vector.tensor_tensor(d_win[t][:, :S], st_win[t][:, :S], gained[:, t, S:], ALU.max)
+            for t in pair:
+                nc.vector.tensor_scalar(gained[:, t, :S], d_win[t][:, :S], gn_rows[:, t:t + 1], None, ALU.mult)
+        half_n3 = sb.tile([P, PACK, S], F32, name="half_n3")
+        for t in TILES:
+            nc.scalar.activation(half_n3[:, t, :], gained[:, t, :].indirect(n3_list[:]), ACT.Copy, scale=0.5)
+
+        d_top = sb.tile([P, PACK], F32, name="d_top")
+        d_bias = sb.tile([P, PACK], F32, name="d_bias")
         ea = sb.tile([P, PACK, S], F32, name="ea")
-        z2f = sb.tile([P, PACK, S], F32, name="z2f")
-        top = sb.tile([P, PACK], F32, name="top")
-        bias = sb.tile([P, PACK], F32, name="bias")
+        for t in TILES:
+            leave_with_bias(d_bank[t], d_win[t], tau_rows, d_top, d_bias, t)
+        for t in TILES:
+            gather_exp(ea[:, t, :], d_win[t], n4_list, tau_rows, d_bias, t)
 
-        zb = sb.tile([P, PACK * S], BF16, name="zb", align_bytes=64)
-        zq = sb.tile([P, S], U32, name="zq", align_bytes=64)
-        zs = sb.tile([P, S], U8, name="zs", align_bytes=64)
+        z_rounded = sb.tile([P, PACK * S], BF16, name="z_rounded", align_bytes=64)
+        z_codes = sb.tile([P, S], U32, name="z_codes", align_bytes=64)
+        z_plane = sb.tile([P, S], U8, name="z_plane", align_bytes=64)
+        half_z2 = sb.tile([P, PACK, S], F32, name="half_z2")
 
-        def ev(t):
-            nc.scalar.copy(ywin[t][:, :S], yb[t][:])
+        def multiply_half_z2(t):
+            nc.vector.scalar_tensor_tensor(half_z2[:, t, :], d_bank[t][:], gm_rows[:, t:t + 1], ea[:, t, :],
+                                           ALU.mult, ALU.mult)
 
-        def g1(t):
-            gather("s", stw[t][:, S:], ywin[t][:], n1_t)
+        nc.vector.tensor_tensor(interleaved(z_rounded), by_lines(gained[:, :, :S]), by_lines(half_n3[:]), ALU.add)
+        multiply_half_z2(0)
+        nc.vector.quantize_mx(out=z_codes[:].bitcast(FP8X4), scales=z_plane[:], in_=z_rounded[:])
+        for t in TILES[1:]:
+            multiply_half_z2(t)
+        z2_codes, z2_plane = quantise_by_halves(half_z2, 2.0, "z2")
 
-        def sub(t):
-            nc.vector.tensor_tensor(stw[t][:, :S], yb[t][:], stw[t][:, S:], ALU.subtract)
+        h_bank = [psum.tile([P, S], F32, name=f"h_bank{t}", tag=f"first{t}") for t in TILES]
+        for t in TILES:
+            product(h_bank[t], w3_dealt, w34_planes, t, z_codes, z_plane, True, False)
+        for t in TILES:
+            product(h_bank[t], w4_dealt, w34_planes[4:P, :], t, z2_codes, z2_plane, False, True)
 
-        def dev(t):
-            leave_with_top(db[t], dwin[t], top, tau_t, bias, t)
-
-        def gg2(t):
-            gather("v" if t < 2 else "s", g2[:, t, :], stw[t][:], n2_t)
-
-        def mx(t):
-            nc.vector.tensor_tensor(zw[:, t, S:], stw[t][:, :S], g2[:, t, :], ALU.max)
-
-        def ts(t):
-            nc.vector.tensor_scalar(zw[:, t, :S], zw[:, t, S:], gn_t[:, t:t + 1], None, ALU.mult)
-
-        def gg3(t):
-            nc.scalar.activation(g3[:, t, :], zw[:, t, :].indirect(n3_t[:]), ACT.Copy, scale=0.5)
-
-        def ex(t):
-            nc.scalar.activation(ea[:, t, :], dwin[t][:].indirect(n4_t[:]), ACT.Exp,
-                                 bias=bias[:, t:t + 1], scale=tau_t[:, t:t + 1])
-
-        def stt(t):
-            nc.vector.scalar_tensor_tensor(z2f[:, t, :], db[t][:], gm2[:, t:t + 1], ea[:, t, :], ALU.mult, ALU.mult)
-
-        def interleave(src, name):
-            tile = sb.tile([P, PACK * S], BF16, name=name, align_bytes=64)
-            nc.vector.tensor_copy(tile[:].rearrange("p (c i t) -> p c t i", i=4, t=PACK),
-                                  src[:].rearrange("p t (c i) -> p c t i", i=4))
-            return tile
-
-        ev(0), ev(1), g1(0), ev(2), g1(1), ev(3), g1(2), g1(3)
-        sub(0), gg2(0), sub(1), mx(0), gg2(1), sub(2), ts(0), mx(1), sub(3), ts(1), dev(0), dev(1)
-        gg2(2), gg2(3), gg3(0), gg3(1)
-        mx(2), mx(3), ts(2), ts(3), dev(2), dev(3)
-        ex(0), ex(1), gg3(2), gg3(3), stt(0), stt(1)
-        nc.vector.tensor_tensor(
-            zb[:].rearrange("p (c i t) -> p c t i", i=4, t=PACK),
-            zw[:, :, :S].rearrange("p t (c i) -> p c t i", i=4),
-            g3[:].rearrange("p t (c i) -> p c t i", i=4), ALU.add)
-        ex(2), ex(3), stt(2)
-        nc.vector.quantize_mx(out=zq[:].bitcast(FP8X4), scales=zs[:], in_=zb[:])
-        stt(3)
-        hb = [psum.tile([P, S], F32, name=f"hb{t}", tag=f"a{t}") for t in range(PACK)]
-        for t in range(PACK):
-            product(hb[t], w3d, w3s, t, zq[:], zs[:], True, False)
-
-        z2b = interleave(z2f, "z2b")
-        z2q = sb.tile([P, S], U32, name="z2q", align_bytes=64)
-        z2s = sb.tile([P, S], U8, name="z2s", align_bytes=64)
-        nc.vector.quantize_mx(out=z2q[:].bitcast(FP8X4), scales=z2s[:], in_=z2b[:])
-        for t in range(PACK):
-            product(hb[t], w4d, w4s, t, z2q[:], z2s[:], False, True)
-
-        hwin = ywin
-        top2 = sb.tile([P, PACK], F32, name="top2")
-        bias2 = sb.tile([P, PACK], F32, name="bias2")
-        g6 = sb.tile([P, PACK, S], F32, name="g6")
+        h_win = y_win
+        h_top = sb.tile([P, PACK], F32, name="h_top")
+        h_bias = sb.tile([P, PACK], F32, name="h_bias")
         ea2 = sb.tile([P, PACK, S], F32, name="ea2")
-        big = sb.tile([P, PACK, S], F32, name="big")
-        res = sb.tile([P, PACK, S], F32, name="res")
+        larger = sb.tile([P, PACK, S], F32, name="larger")
+        result = sb.tile([P, PACK, S], F32, name="result")
         out_rows = out_0.rearrange("(p t) c -> p t c", t=PACK)
-        for t in range(PACK):
-            leave_with_top(hb[t], hwin[t], top2, tau2_t, bias2, t)
-        for t in range(PACK):
-            gather("v" if t == 3 else "s", g6[:, t, :], hwin[t][:], n6_t)
-            nc.scalar.activation(ea2[:, t, :], hwin[t][:].indirect(n5_t[:]), ACT.Exp,
-                                 bias=bias2[:, t:t + 1], scale=tau2_t[:, t:t + 1])
-            nc.vector.scalar_tensor_tensor(big[:, t, :], ea2[:, t, :], 2.0, hb[t][:], ALU.mult, ALU.max)
-            nc.vector.scalar_tensor_tensor(res[:, t, :], g6[:, t, :], -0.5, big[:, t, :], ALU.mult, ALU.add)
-            nc.sync.dma_start(out_rows[:, t, :], res[:, t, :])
+        (early, late), second_pair = PAIRS
+        from_n6 = [ea2[:, t, :] if t == late else sb.tile([P, S], F32, name=f"from_n6_{t}")[:] for t in TILES]
 
-        ob = interleave(res, "ob")
-        oq = sb.tile([P, S], U32, name="oq", align_bytes=64)
-        osc = sb.tile([P, S], U8, name="osc", align_bytes=64)
-        nc.vector.quantize_mx(out=oq[:].bitcast(FP8X4), scales=osc[:], in_=ob[:])
-        nc.sync.dma_start(out_1[0].rearrange("p n t -> p (n t)").bitcast(I32), oq[:].bitcast(I32))
+        def gather_minus_half(t):
+            nc.scalar.activation(from_n6[t], h_win[t][:].indirect(n6_list[:]), ACT.Copy, scale=-0.5)
+
+        def add_and_store(engine, t):
+            engine.tensor_tensor(result[:, t, :], from_n6[t], larger[:, t, :], ALU.add)
+            nc.sync.dma_start(out_rows[:, t, :], result[:, t, :])
+
+        for t in TILES:
+            leave_with_bias(h_bank[t], h_win[t], tau2_rows, h_top, h_bias, t)
+        gather_minus_half(early)
+        for t in TILES:
+            gather_exp(ea2[:, t, :], h_win[t], n5_list, tau2_rows, h_bias, t)
+        for t in second_pair:
+            nc.vector.tensor_copy(from_n6[t], h_win[t][:].indirect(n6_list[:]))
+        for t in TILES:
+            nc.vector.scalar_tensor_tensor(larger[:, t, :], ea2[:, t, :], 2.0, h_bank[t][:], ALU.mult, ALU.max)
+        gather_minus_half(late)
+        add_and_store(nc.gpsimd, early)
+        for t in second_pair:
+            nc.vector.scalar_tensor_tensor(result[:, t, :], from_n6[t], -0.5, larger[:, t, :], ALU.mult, ALU.add)
+            nc.sync.dma_start(out_rows[:, t, :], result[:, t, :])
+        add_and_store(nc.vector, late)
+
+        out_codes, out_plane = quantise_by_halves(result, 1.0, "out")
+        nc.sync.dma_start(out_1[0].rearrange("p n t -> p (n t)").bitcast(I32), out_codes[:].bitcast(I32))
         for q in range(QUADS):
-            engine = nc.scalar if q % 2 == 0 else nc.sync
-            engine.dma_start(out_2[0, 4 * q:4 * q + 4, :].bitcast(I32), osc[32 * q:32 * q + 4, :].bitcast(I32))
+            queue = nc.scalar if q % 2 == 0 else nc.sync
+            queue.dma_start(out_2[0, 4 * q:4 * q + 4, :].bitcast(I32), out_plane[32 * q:32 * q + 4, :].bitcast(I32))

@@ -40,13 +40,13 @@ def tile_picked_hjointhreeepkecl_none_po_kernel(
             nc.sync.dma_start(tile[:], src)
             return tile
 
-        def load_words(src, width, name):
-            tile = sb.tile([P, width], U32, name=name, tag=name, align_bytes=64)
+        def load_words(src, width, name, tag):
+            tile = sb.tile([P, width], U32, name=name, tag=tag, align_bytes=64)
             nc.sync.dma_start(tile[:].bitcast(I32), src[0].rearrange("p n t -> p (n t)").bitcast(I32))
             return tile
 
         def load_row_values(queue, src, name):
-            tile = sb.tile([P, PACK], F32, name=name)
+            tile = sb.tile([P, PACK], F32, name=name, tag=name, align_bytes=64)
             queue.dma_start(tile[:], src.rearrange("(p t) o -> p (t o)", t=PACK))
             return tile
 
@@ -84,23 +84,22 @@ def tile_picked_hjointhreeepkecl_none_po_kernel(
         fill_scale_rows(x_rows, x_scales, shared_queues)
         offs_list = load_list(offs, "offs_list")
         hz_list = load_list(hz, "hz_list")
-        x_table = load_words(x_words, T, "x_table")
+        x_table = load_words(x_words, T, "x_table", "x_table")
         w1_rows = sb.tile([P, H], U8, name="w1_rows", align_bytes=64)
         fill_scale_rows(w1_rows, w1_scales, shared_queues)
         n1_list = load_list(n1, "n1_list")
-        w1_raw = load_words(w1_words, H, "w1_raw")
-        w2_raw = load_words(w2_words, H, "w2_raw")
+        w1_raw = load_words(w1_words, H, "w1_raw", "w1_raw")
+        w2_raw = load_words(w2_words, H, "w2_raw", "w2_raw")
         n2_list = load_list(n2, "n2_list")
         w2_rows = sb.tile([P, H], U8, name="w2_rows", align_bytes=64)
         fill_scale_rows(w2_rows, w2_scales, (nc.sync,) * QUADS)
-        w3_raw = load_words(w3_words, N, "w3_raw")
-        w4_raw = load_words(w4_words, N, "w4_raw")
+        w3_raw = load_words(w3_words, N, "w3_raw", "w3_raw")
         tau_rows = load_row_values(nc.gpsimd, tau, "tau_rows")
         gn_rows = load_row_values(nc.gpsimd, gn, "gn_rows")
         gm_rows = load_row_values(nc.gpsimd, gm, "gm_rows")
 
         y_win = [sb.tile([P, 2 * S], F32, name=f"y_win{t}") for t in TILES]
-        d_win = [sb.tile([P, 2 * S], F32, name=f"d_win{t}", align_bytes=64) for t in TILES]
+        d_win = [sb.tile([P, 2 * S], F32, name=f"d_win{t}", tag=f"d_win{t}", align_bytes=64) for t in TILES]
         for tile in y_win + d_win:
             nc.vector.memset(tile[:, S:], 0.0)
 
@@ -132,10 +131,9 @@ def tile_picked_hjointhreeepkecl_none_po_kernel(
         tau2_rows = load_row_values(nc.sync, tau2, "tau2_rows")
 
         w3_dealt = deal_words(w3_raw, "w3_dealt")
-        w4_dealt = deal_words(w4_raw, "w4_dealt")
+        w4_raw = load_words(w4_words, N, "w4_raw", "w1_raw")
         load_scale_rows(w1_rows, w3_scales, 0)
         load_scale_rows(w1_rows, w4_scales, 4)
-        w34_planes = deal_bytes(w1_rows, "w34_planes", "w34_planes")
 
         def product(bank, words, plane, t, moving, moving_plane, start, stop):
             cols = slice(t * P, (t + 1) * P)
@@ -164,16 +162,8 @@ def tile_picked_hjointhreeepkecl_none_po_kernel(
         def by_lines(tiles):
             return tiles.rearrange("p t (c i) -> p c t i", i=LINE)
 
-        def quantise_by_halves(src, factor, name):
-            codes = sb.tile([P, S], U32, name=name + "_codes", align_bytes=64)
-            plane = sb.tile([P, S], U8, name=name + "_plane", align_bytes=64)
-            low = sb.tile([P, PACK * S // 2], BF16, name=name + "_low", align_bytes=64)
-            nc.vector.tensor_scalar(interleaved(low), by_lines(src[:, :, :S // 2]), factor, None, ALU.mult)
-            high = sb.tile([P, PACK * S // 2], BF16, name=name + "_high", align_bytes=64)
-            nc.scalar.activation(interleaved(high), by_lines(src[:, :, S // 2:]), ACT.Copy, scale=factor)
-            for rounded, cols in ((low, slice(0, S // 2)), (high, slice(S // 2, S))):
-                nc.vector.quantize_mx(out=codes[:, cols].bitcast(FP8X4), scales=plane[:, cols], in_=rounded[:])
-            return codes, plane
+        def quantise(rounded, codes, plane):
+            nc.vector.quantize_mx(out=codes.bitcast(FP8X4), scales=plane, in_=rounded[:])
 
         st_win = [sb.tile([P, 2 * S], F32, name=f"st_win{t}") for t in TILES]
         for a, b in PAIRS:
@@ -192,6 +182,7 @@ def tile_picked_hjointhreeepkecl_none_po_kernel(
                 nc.vector.tensor_tensor(d_win[t][:, :S], st_win[t][:, :S], gained[:, t, S:], ALU.max)
             for t in pair:
                 nc.vector.tensor_scalar(gained[:, t, :S], d_win[t][:, :S], gn_rows[:, t:t + 1], None, ALU.mult)
+        w34_planes = deal_bytes(w1_rows, "w34_planes", "gn_rows")
         half_n3 = sb.tile([P, PACK, S], F32, name="half_n3")
         for t in TILES:
             nc.scalar.activation(half_n3[:, t, :], gained[:, t, :].indirect(n3_list[:]), ACT.Copy, scale=0.5)
@@ -204,6 +195,9 @@ def tile_picked_hjointhreeepkecl_none_po_kernel(
         for t in TILES:
             gather_exp(ea[:, t, :], d_win[t], n4_list, tau_rows, d_bias, t)
 
+        w4_dealt = sb.tile([P, N], U32, name="w4_dealt", tag="d_win3", align_bytes=64)
+        nc.scalar.copy(*dealt_views(w4_dealt, w4_raw))
+
         z_rounded = sb.tile([P, PACK * S], BF16, name="z_rounded", align_bytes=64)
         z_codes = sb.tile([P, S], U32, name="z_codes", align_bytes=64)
         z_plane = sb.tile([P, S], U8, name="z_plane", align_bytes=64)
@@ -215,10 +209,14 @@ def tile_picked_hjointhreeepkecl_none_po_kernel(
 
         nc.vector.tensor_tensor(interleaved(z_rounded), by_lines(gained[:, :, :S]), by_lines(half_n3[:]), ALU.add)
         multiply_half_z2(0)
-        nc.vector.quantize_mx(out=z_codes[:].bitcast(FP8X4), scales=z_plane[:], in_=z_rounded[:])
+        quantise(z_rounded, z_codes[:], z_plane[:])
         for t in TILES[1:]:
             multiply_half_z2(t)
-        z2_codes, z2_plane = quantise_by_halves(half_z2, 2.0, "z2")
+        z2_rounded = sb.tile([P, PACK * S], BF16, name="z2_rounded", align_bytes=64)
+        z2_codes = sb.tile([P, S], U32, name="z2_codes", align_bytes=64)
+        z2_plane = sb.tile([P, S], U8, name="z2_plane", align_bytes=64)
+        nc.vector.tensor_scalar(interleaved(z2_rounded), by_lines(half_z2[:]), 2.0, None, ALU.mult)
+        quantise(z2_rounded, z2_codes[:], z2_plane[:])
 
         h_bank = [psum.tile([P, S], F32, name=f"h_bank{t}", tag=f"first{t}") for t in TILES]
         for t in TILES:
@@ -259,7 +257,15 @@ def tile_picked_hjointhreeepkecl_none_po_kernel(
             nc.sync.dma_start(out_rows[:, t, :], result[:, t, :])
         add_and_store(nc.vector, late)
 
-        out_codes, out_plane = quantise_by_halves(result, 1.0, "out")
+        low, high = slice(0, S // 2), slice(S // 2, S)
+        out_codes = sb.tile([P, S], U32, name="out_codes", align_bytes=64)
+        out_plane = sb.tile([P, S], U8, name="out_plane", align_bytes=64)
+        out_low = sb.tile([P, PACK * S // 2], BF16, name="out_low", align_bytes=64)
+        nc.vector.tensor_copy(interleaved(out_low), by_lines(result[:, :, low]))
+        out_high = sb.tile([P, PACK * S // 2], BF16, name="out_high", align_bytes=64)
+        nc.scalar.copy(interleaved(out_high), by_lines(result[:, :, high]))
+        quantise(out_low, out_codes[:, low], out_plane[:, low])
+        quantise(out_high, out_codes[:, high], out_plane[:, high])
         nc.sync.dma_start(out_1[0].rearrange("p n t -> p (n t)").bitcast(I32), out_codes[:].bitcast(I32))
         for q in range(QUADS):
             queue = nc.scalar if q % 2 == 0 else nc.sync

from contextlib import ExitStack

import concourse.mybir as mybir

K, T, S, N, H = 512, 2048, 256, 512, 512
FLOPS = 2 * (2 * K * H * S) + 2 * (2 * H * N * S)

F32 = mybir.dt.float32
BF16 = mybir.dt.bfloat16
I32 = mybir.dt.int32
U32 = mybir.dt.uint32
U16 = mybir.dt.uint16
U8 = mybir.dt.uint8
FP8X4 = mybir.dt.float8_e4m3fn_x4
ALU = mybir.AluOpType
ACT = mybir.ActivationFunctionType

P = 128
PACK = 4
QUADS = 4
LINE = 4
FILL = 8
TILES = range(PACK)
PAIRS = ((0, 1), (2, 3))


def tile_picked_hjointhreeepkecl_none_po_kernel(
    tc, x_words, x_scales, w1_words, w1_scales, w2_words, w2_scales, tau, gn, gm,
    w3_words, w3_scales, w4_words, w4_scales, tau2, offs, hz, n1, n2, n3, n4, n5, n6,
    out_0, out_1, out_2,
):
    nc = tc.nc
    with ExitStack() as ctx:
        lists = ctx.enter_context(tc.tile_pool(name="lists", bufs=1))
        sb = ctx.enter_context(tc.tile_pool(name="sb", bufs=1))
        psum = ctx.enter_context(tc.psum_pool(name="psum", bufs=1))

        def load_list(src, name):
            tile = lists.tile([P, S // 16], U16, name=name)
            nc.sync.dma_start(tile[:], src)
            return tile

        def load_words(src, width, name, tag):
            tile = sb.tile([P, width], U32, name=name, tag=tag, align_bytes=64)
            nc.sync.dma_start(tile[:].bitcast(I32), src[0].rearrange("p n t -> p (n t)").bitcast(I32))
            return tile

        def load_row_values(queue, src, name):
            tile = sb.tile([P, PACK], F32, name=name, tag=name, align_bytes=64)
            queue.dma_start(tile[:], src.rearrange("(p t) o -> p (t o)", t=PACK))
            return tile

        def fill_scale_rows(tile, src, queues):
            for q, queue in enumerate(queues):
                rows = src[0, 4 * q:4 * q + 4, :].bitcast(I32)
                queue.dma_start(tile[32 * q:32 * (q + 1), :].bitcast(I32),
                                rows.unsqueeze(0).broadcast_to([FILL] + list(rows.shape)))

        def load_scale_rows(tile, src, first):
            for q in range(QUADS):
                nc.sync.dma_start(tile[32 * q + first:32 * q + first + 4, :].bitcast(I32),
                                  src[0, 4 * q:4 * q + 4, :].bitcast(I32))

        def dealt_views(dealt, raw):
            return (dealt[:].rearrange("p (t a i) -> p a t i", t=PACK, i=LINE),
                    raw[:].rearrange("p (a i t) -> p a t i", t=PACK, i=LINE))

        def deal_words(raw, name):
            tile = sb.tile([P, H], U32, name=name, align_bytes=64)
            nc.gpsimd.tensor_copy(*dealt_views(tile, raw))
            return tile

        def deal_bytes(raw, name, tag):
            tile = sb.tile([P, H], U8, name=name, tag=tag, align_bytes=64)
            nc.gpsimd.tensor_copy(tile[:].rearrange("p (t m) -> p t m", t=PACK),
                                  raw[:].rearrange("p (m t) -> p t m", t=PACK))
            return tile

        def gather_packed(out, window, offsets):
            nc.vector.tensor_copy(out[:], window[:].indirect(offsets[:]))

        shared_queues = (nc.scalar, nc.scalar, nc.scalar, nc.sync)
        x_rows = sb.tile([P, T], U8, name="x_rows", align_bytes=64)
        fill_scale_rows(x_rows, x_scales, shared_queues)
        offs_list = load_list(offs, "offs_list")
        hz_list = load_list(hz, "hz_list")
        x_table = load_words(x_words, T, "x_table", "x_table")
        w1_rows = sb.tile([P, H], U8, name="w1_rows", align_bytes=64)
        fill_scale_rows(w1_rows, w1_scales, shared_queues)
        n1_list = load_list(n1, "n1_list")
        w1_raw = load_words(w1_words, H, "w1_raw", "w1_raw")
        w2_raw = load_words(w2_words, H, "w2_raw", "w2_raw")
        n2_list = load_list(n2, "n2_list")
        w2_rows = sb.tile([P, H], U8, name="w2_rows", align_bytes=64)
        fill_scale_rows(w2_rows, w2_scales, (nc.sync,) * QUADS)
        w3_raw = load_words(w3_words, N, "w3_raw", "w3_raw")
        tau_rows = load_row_values(nc.gpsimd, tau, "tau_rows")
        gn_rows = load_row_values(nc.gpsimd, gn, "gn_rows")
        gm_rows = load_row_values(nc.gpsimd, gm, "gm_rows")

        y_win = [sb.tile([P, 2 * S], F32, name=f"y_win{t}") for t in TILES]
        d_win = [sb.tile([P, 2 * S], F32, name=f"d_win{t}", tag=f"d_win{t}", align_bytes=64) for t in TILES]
        for tile in y_win + d_win:
            nc.vector.memset(tile[:, S:], 0.0)

        picked_plane = sb.tile([P, S], U8, name="picked_plane", align_bytes=64)
        gather_packed(picked_plane, x_rows, offs_list)
        w1_plane = deal_bytes(w1_rows, "w1_plane", "w1_plane")
        picked_words = sb.tile([P, S], U32, name="picked_words", align_bytes=64)
        gather_packed(picked_words, x_table, offs_list)
        w1_dealt = sb.tile([P, H], U32, name="w1_dealt", align_bytes=64)
        dealt_view, raw_view = dealt_views(w1_dealt, w1_raw)
        for a, b in PAIRS:
            nc.scalar.copy(dealt_view[:, :, a:b + 1, :], raw_view[:, :, a:b + 1, :])

        hashed_bytes = sb.tile([P, S], U8, name="hashed_bytes", align_bytes=64)
        gather_packed(hashed_bytes, x_rows, hz_list)
        hashed_plane = sb.tile([P, S], U8, name="hashed_plane", align_bytes=64)
        nc.vector.tensor_copy(hashed_plane[:], hashed_bytes[:])
        for r in (2, 3):
            nc.sync.dma_start(hashed_plane[r:P:32, :].bitcast(I32), hashed_bytes[16 + r:P:32, :].bitcast(I32))
        hashed_words = sb.tile([P, S], U32, name="hashed_words", align_bytes=64)
        gather_packed(hashed_words, x_table, hz_list)
        w2_dealt = deal_words(w2_raw, "w2_dealt")
        w2_plane = deal_bytes(w2_rows, "w2_plane", "w2_raw")

        n3_list = load_list(n3, "n3_list")
        n4_list = load_list(n4, "n4_list")
        n6_list = load_list(n6, "n6_list")
        n5_list = load_list(n5, "n5_list")
        tau2_rows = load_row_values(nc.sync, tau2, "tau2_rows")

        w3_dealt = deal_words(w3_raw, "w3_dealt")
        w4_raw = load_words(w4_words, N, "w4_raw", "w1_raw")
        load_scale_rows(w1_rows, w3_scales, 0)
        load_scale_rows(w1_rows, w4_scales, 4)

        def product(bank, words, plane, t, moving, moving_plane, start, stop):
            cols = slice(t * P, (t + 1) * P)
            nc.tensor.matmul_mx(bank[:], lhsT=words[:, cols].bitcast(FP8X4), lhsT_scale=plane[:, cols],
                                rhs=moving[:].bitcast(FP8X4), rhs_scale=moving_plane[:], start=start, stop=stop)

        y_bank = [psum.tile([P, S], F32, name=f"y_bank{t}", tag=f"first{t}") for t in TILES]
        d_bank = [psum.tile([P, S], F32, name=f"d_bank{t}") for t in TILES]
        for t in TILES:
            product(y_bank[t], w1_dealt, w1_plane, t, picked_words, picked_plane, True, True)
        for t in TILES:
            product(d_bank[t], w2_dealt, w2_plane, t, hashed_words, hashed_plane, True, True)

        def leave_with_bias(bank, win, rate, top, bias, t):
            col = slice(t, t + 1)
            nc.vector.tensor_scalar(win[:, :S], bank[:], 1.0, None, ALU.mult, ALU.max, accum_out=top[:, col])
            nc.gpsimd.tensor_scalar(bias[:, col], top[:, col], rate[:, col], -1.0, ALU.mult, ALU.mult)

        def gather_exp(out, win, offsets, rate, bias, t):
            nc.scalar.activation(out, win[:].indirect(offsets[:]), ACT.Exp,
                                 bias=bias[:, t:t + 1], scale=rate[:, t:t + 1])

        def interleaved(tile):
            return tile[:].rearrange("p (c i t) -> p c t i", i=LINE, t=PACK)

        def by_lines(tiles):
            return tiles.rearrange("p t (c i) -> p c t i", i=LINE)

        def quantise(rounded, codes, plane):
            nc.vector.quantize_mx(out=codes.bitcast(FP8X4), scales=plane, in_=rounded[:])

        st_win = [sb.tile([P, 2 * S], F32, name=f"st_win{t}") for t in TILES]
        for a, b in PAIRS:
            nc.scalar.copy(y_win[a][:, :S], y_bank[a][:])
            nc.scalar.copy(y_win[b][:, :S], y_bank[b][:])
            nc.scalar.activation(st_win[a][:, S:], y_win[a][:].indirect(n1_list[:]), ACT.Copy)
            nc.vector.tensor_copy(st_win[b][:, S:], y_win[b][:].indirect(n1_list[:]))
            for t in (a, b):
                nc.vector.tensor_tensor(st_win[t][:, :S], y_bank[t][:], st_win[t][:, S:], ALU.subtract)

        gained = sb.tile([P, PACK, 2 * S], F32, name="gained")
        for t in TILES:
            nc.scalar.activation(gained[:, t, S:], st_win[t][:].indirect(n2_list[:]), ACT.Copy)
        for pair in PAIRS:
            for t in pair:
                nc.vector.tensor_tensor(d_win[t][:, :S], st_win[t][:, :S], gained[:, t, S:], ALU.max)
            for t in pair:
                nc.vector.tensor_scalar(gained[:, t, :S], d_win[t][:, :S], gn_rows[:, t:t + 1], None, ALU.mult)
        w34_planes = deal_bytes(w1_rows, "w34_planes", "gn_rows")
        half_n3 = sb.tile([P, PACK, S], F32, name="half_n3")
        for t in TILES:
            nc.scalar.activation(half_n3[:, t, :], gained[:, t, :].indirect(n3_list[:]), ACT.Copy, scale=0.5)

        d_top = sb.tile([P, PACK], F32, name="d_top")
        d_bias = sb.tile([P, PACK], F32, name="d_bias")
        ea = sb.tile([P, PACK, S], F32, name="ea")
        for t in TILES:
            leave_with_bias(d_bank[t], d_win[t], tau_rows, d_top, d_bias, t)
        for t in TILES:
            gather_exp(ea[:, t, :], d_win[t], n4_list, tau_rows, d_bias, t)

        w4_dealt = sb.tile([P, N], U32, name="w4_dealt", tag="d_win3", align_bytes=64)
        nc.scalar.copy(*dealt_views(w4_dealt, w4_raw))

        z_rounded = sb.tile([P, PACK * S], BF16, name="z_rounded", align_bytes=64)
        z_codes = sb.tile([P, S], U32, name="z_codes", align_bytes=64)
        z_plane = sb.tile([P, S], U8, name="z_plane", align_bytes=64)
        half_z2 = sb.tile([P, PACK, S], F32, name="half_z2")

        def multiply_half_z2(t):
            nc.vector.scalar_tensor_tensor(half_z2[:, t, :], d_bank[t][:], gm_rows[:, t:t + 1], ea[:, t, :],
                                           ALU.mult, ALU.mult)

        nc.vector.tensor_tensor(interleaved(z_rounded), by_lines(gained[:, :, :S]), by_lines(half_n3[:]), ALU.add)
        multiply_half_z2(0)
        quantise(z_rounded, z_codes[:], z_plane[:])
        for t in TILES[1:]:
            multiply_half_z2(t)
        z2_rounded = sb.tile([P, PACK * S], BF16, name="z2_rounded", align_bytes=64)
        z2_codes = sb.tile([P, S], U32, name="z2_codes", align_bytes=64)
        z2_plane = sb.tile([P, S], U8, name="z2_plane", align_bytes=64)
        nc.vector.tensor_scalar(interleaved(z2_rounded), by_lines(half_z2[:]), 2.0, None, ALU.mult)
        quantise(z2_rounded, z2_codes[:], z2_plane[:])

        h_bank = [psum.tile([P, S], F32, name=f"h_bank{t}", tag=f"first{t}") for t in TILES]
        for t in TILES:
            product(h_bank[t], w3_dealt, w34_planes, t, z_codes, z_plane, True, False)
        for t in TILES:
            product(h_bank[t], w4_dealt, w34_planes[4:P, :], t, z2_codes, z2_plane, False, True)

        h_win = y_win
        h_top = sb.tile([P, PACK], F32, name="h_top")
        h_bias = sb.tile([P, PACK], F32, name="h_bias")
        ea2 = sb.tile([P, PACK, S], F32, name="ea2")
        larger = sb.tile([P, PACK, S], F32, name="larger")
        result = sb.tile([P, PACK, S], F32, name="result")
        out_rows = out_0.rearrange("(p t) c -> p t c", t=PACK)
        (early, late), second_pair = PAIRS
        from_n6 = [ea2[:, t, :] if t == late else sb.tile([P, S], F32, name=f"from_n6_{t}")[:] for t in TILES]

        def gather_minus_half(t):
            nc.scalar.activation(from_n6[t], h_win[t][:].indirect(n6_list[:]), ACT.Copy, scale=-0.5)

        def add_and_store(engine, t):
            engine.tensor_tensor(result[:, t, :], from_n6[t], larger[:, t, :], ALU.add)
            nc.sync.dma_start(out_rows[:, t, :], result[:, t, :])

        for t in TILES:
            leave_with_bias(h_bank[t], h_win[t], tau2_rows, h_top, h_bias, t)
        gather_minus_half(early)
        for t in TILES:
            gather_exp(ea2[:, t, :], h_win[t], n5_list, tau2_rows, h_bias, t)
        for t in second_pair:
            nc.vector.tensor_copy(from_n6[t], h_win[t][:].indirect(n6_list[:]))
        for t in TILES:
            nc.vector.scalar_tensor_tensor(larger[:, t, :], ea2[:, t, :], 2.0, h_bank[t][:], ALU.mult, ALU.max)
        gather_minus_half(late)
        add_and_store(nc.gpsimd, early)
        for t in second_pair:
            nc.vector.scalar_tensor_tensor(result[:, t, :], from_n6[t], -0.5, larger[:, t, :], ALU.mult, ALU.add)
            nc.sync.dma_start(out_rows[:, t, :], result[:, t, :])
        add_and_store(nc.vector, late)

        low, high = slice(0, S // 2), slice(S // 2, S)
        out_codes = sb.tile([P, S], U32, name="out_codes", align_bytes=64)
        out_plane = sb.tile([P, S], U8, name="out_plane", align_bytes=64)
        out_low = sb.tile([P, PACK * S // 2], BF16, name="out_low", align_bytes=64)
        nc.vector.tensor_copy(interleaved(out_low), by_lines(result[:, :, low]))
        out_high = sb.tile([P, PACK * S // 2], BF16, name="out_high", align_bytes=64)
        nc.scalar.copy(interleaved(out_high), by_lines(result[:, :, high]))
        quantise(out_low, out_codes[:, low], out_plane[:, low])
        quantise(out_high, out_codes[:, high], out_plane[:, high])
        nc.sync.dma_start(out_1[0].rearrange("p n t -> p (n t)").bitcast(I32), out_codes[:].bitcast(I32))
        for q in range(QUADS):
            queue = nc.scalar if q % 2 == 0 else nc.sync
            queue.dma_start(out_2[0, 4 * q:4 * q + 4, :].bitcast(I32), out_plane[32 * q:32 * q + 4, :].bitcast(I32))
